import numpy as np, ml_dtypes
CORES = [21,29,37,45,53,61,69,77,85]
N = 9
import mx_ref
NC, KT = 256, 2
BF = ml_dtypes.bfloat16
def setup_inputs(rng):
    def f(*shape):
        return mx_ref.flush((rng.standard_normal(shape, dtype=np.float32) * np.exp2(rng.integers(-2, 3, shape[:-1] + (1,)))).astype(BF))
    return {"w": f(N, 128, KT * 512), "x": f(N, 128, KT * 4 * NC)}
def setup_inputs_blocks(rng):
    d = setup_inputs(rng)
    for k in ("w", "x"): d[k] = mx_ref.spread(d[k], rng, 4)
    return d
def setup_inputs_wide(rng):
    d = setup_inputs(rng)
    for k in ("w", "x"): d[k] = mx_ref.flush((d[k].astype(np.float32) * np.exp2(rng.integers(-8, 9, (N, 1, 1))).astype(np.float32)).astype(BF))
    return d
def reference(w, x):
    QW = [[mx_ref.quantize(w[r][:, 512 * t:512 * t + 512]) for t in range(KT)] for r in range(N)]
    QX = [[mx_ref.quantize(x[j][:, 4 * NC * t:4 * NC * t + 4 * NC]) for t in range(KT)] for j in range(N)]
    y = np.zeros((N, 128, N * NC), np.float32)
    for r in range(N):
        for j in range(N):
            for t in range(KT):
                p = mx_ref.matmul(QW[r][t], QX[j][t])
                y[r][:, NC * j:NC * j + NC] = p if t == 0 else y[r][:, NC * j:NC * j + NC] + p
    return {"y": y}

from concourse.bass import DstId, RemoteDMATransfer
from concourse.mybir import dt

N = 9
KT = 2
NC = 256
BW = KT * NC
NSIM = 96
BANKS = 8

SCRATCH = {
    "xb": ("sbuf", [128, KT * 4 * NC], "bfloat16"),
    "wb": ("sbuf", [128, KT * 512], "bfloat16"),
    "wq": ("sbuf", [128, KT * 128], "float8_e4m3fn_x4"),
    "ws": ("sbuf", [128, KT * 128], "uint8"),
    "xq": ("sbuf", [128, N * BW], "float8_e4m3fn_x4"),
    "xs": ("sbuf", [128, N * BW], "uint8"),
    "ps": ("psum", [128, 512 * BANKS], "float32"),
    "yb": ("sbuf", [128, N * NC], "float32"),
}
PIECES = [("as", "xs"), ("ac", "xq")]
SEMAPHORES = (["lx0", "lx1", "lw", "qx", "qw", "sent", "sta", "stb"]
              + ["%s%d" % (p[0], j) for p in PIECES for j in range(N)]
              + ["mm%d" % j for j in range(N)] + ["ev%d" % j for j in range(N)])


def _engines(mask):
    return bin(mask).count("1")


def _groups(src, dsts, topo):
    off = [d for d in dsts if topo.chip(d) != topo.chip(src)]
    on = [d for d in dsts if topo.chip(d) == topo.chip(src)]
    out = []
    if off:
        m_off = topo.mask(src, off[0])
        out.append((m_off, off))
        if on:
            out.append((topo.mask(src, on[0]) & ~m_off, on))
    elif on:
        out.append((topo.mask(src, on[0]), on))
    return out


def _routes(cores, topo):
    rank_at = {topo.chip(c): c for c in cores}
    chips = sorted({topo.chip(c) for c in range(NSIM)})
    on_chip = {ch: [c for c in range(NSIM) if topo.chip(c) == ch] for ch in chips}
    mate = {ch: [m for m in chips if topo.mates(ch, m)][0] for ch in chips}
    used = sorted(set(rank_at) | {mate[ch] for ch in rank_at})

    def owners(ch, die):
        return [c for c in on_chip[ch] if topo.die(c) == die and topo.may_write(c, on_chip[mate[ch]][0])]

    first, relay = {}, {}
    for j, r in enumerate(cores):
        ch = topo.chip(r)
        ring = [d for d in used if d == ch or topo.same_plane(ch, d)]
        p, n = ring.index(ch), len(ring)
        home = topo.die(r)
        far = [topo.die(c) for c in on_chip[ch] if topo.die(c) != home][0]
        half = n // 2

        def target(k):
            d = ring[(p + k) % n]
            die, idx = (home, k - 1) if k <= half else (far, k - 1 - half)
            if mate[d] not in rank_at:
                return rank_at[d]
            own = owners(d, die)
            f = own[idx % len(own)]
            relay.setdefault(f, []).append((j, [rank_at[mate[d]]] + ([rank_at[d]] if d in rank_at else [])))
            return f

        helpers = owners(ch, far)
        first.setdefault(r, []).extend((j, [h]) for h in helpers)
        first[r].extend((j, [target(k)]) for k in range(1, half + 1))
        for i, h in enumerate(helpers):
            dsts = [target(k) for k in range(half + 1, n) if (k - 1 - half) % len(helpers) == i]
            if i == 0 and mate[ch] in rank_at:
                dsts.append(rank_at[mate[ch]])
            first.setdefault(h, []).extend((j, [d]) for d in dsts)
    return {c: first.get(c, []) + relay.get(c, []) for c in set(first) | set(relay)}


def _plan(cores, topo):
    sends = _routes(cores, topo)
    count, eta = {}, {(c, j): 0.0 for j, c in enumerate(cores)}
    free, todo = {}, {c: list(s) for c, s in sends.items()}
    moved = True
    while moved:
        moved = False
        for c in sorted(todo):
            while todo[c] and (c, todo[c][0][0]) in eta:
                j, dsts = todo[c].pop(0)
                t0 = max(free.get(c, 0.0), eta[(c, j)])
                for m, ds in _groups(c, dsts, topo):
                    t = t0
                    for d in ds:
                        t += 8.0 / _engines(m)
                        eta[(d, j)] = t + 1.0
                        count[(d, j)] = _engines(m)
                    free[c] = max(free.get(c, 0.0), t)
                moved = True
    return sends, count, eta


def rank_program(g, core, T, topo):
    cores = list(T.cores)
    sends, count, eta = _plan(cores, topo)
    rank = T.rank_of(core)
    mine = sends.get(core, [])
    if rank is None and not mine:
        return
    sem = T.sem

    if rank is not None:
        g.sync.dma_start(T.xb[:, 0:4 * NC], T.x[:, 0:4 * NC]).then_inc(sem.lx0, 16)
        g.scalar.dma_start(T.xb[:, 4 * NC:8 * NC], T.x[:, 4 * NC:8 * NC]).then_inc(sem.lx1, 16)
        g.sync.dma_start(T.wb[:], T.w[:]).then_inc(sem.lw, 16)
        for t in range(KT):
            g.vector.wait_ge(sem["lx%d" % t], 16)
            a = BW * rank + NC * t
            g.vector.quantize_mx(T.xq[:, a:a + NC], T.xs[:, a:a + NC],
                                 T.xb[:, 4 * NC * t:4 * NC * (t + 1)]).then_inc(sem.qx, 1)
        g.vector.wait_ge(sem.lw, 16)
        for t in range(KT):
            g.vector.quantize_mx(T.wq[:, 128 * t:128 * (t + 1)], T.ws[:, 128 * t:128 * (t + 1)],
                                 T.wb[:, 512 * t:512 * (t + 1)]).then_inc(sem.qw, 1)

    total = 0
    for j, dsts in mine:
        for name, buf in PIECES:
            view = T[buf][:, BW * j:BW * (j + 1)]
            if buf == "xq":
                view = view.bitcast(dt.uint8)
            if j == rank:
                g.wait_ge(sem.qx, KT)
            else:
                g.wait_ge(sem["%s%d" % (name, j)], count[(core, j)])
            transfers = []
            for m, ds in _groups(core, dsts, topo):
                ids = [DstId(rid=topo.addr(d)[0], pnc=topo.addr(d)[1]) for d in ds]
                transfers.append(RemoteDMATransfer(dst_ids=ids, dma_engine_mask=m, remote_sem=sem["%s%d" % (name, j)],
                                                   srcs=[view], dsts=[view for d in ds], alu_op=0))
                total += _engines(m)
            g.remote_dma_fused(transfers, local_sem=sem.sent)

    if rank is not None:
        order = sorted(range(N), key=lambda j: (eta[(core, j)], j))
        stores = {"sta": 0, "stb": 0}
        g.tensor.wait_ge(sem.qw, KT)
        for k, j in enumerate(order):
            if j == rank:
                g.tensor.wait_ge(sem.qx, KT)
            else:
                for name, buf in PIECES:
                    g.tensor.wait_ge(sem["%s%d" % (name, j)], count[(core, j)])
            if k >= BANKS:
                g.tensor.wait_ge(sem["ev%d" % order[k - BANKS]], 1)
            bank = T.ps[:, 512 * (k % BANKS):512 * (k % BANKS) + NC]
            for t in range(KT):
                a = BW * j + NC * t
                mm = g.tensor.matmul_mx(bank, T.wq[:, 128 * t:128 * (t + 1)], T.ws[:, 128 * t:128 * (t + 1)],
                                        T.xq[:, a:a + NC], T.xs[:, a:a + NC], t == 0, t == KT - 1)
            mm.then_inc(sem["mm%d" % j], 1)
            g.vector.wait_ge(sem["mm%d" % j], 1)
            g.vector.tensor_copy(T.yb[:, NC * j:NC * (j + 1)], bank).then_inc(sem["ev%d" % j], 1)
            q, st = ((g.sync, "sta"), (g.scalar, "stb"))[k % 2]
            q.wait_ge(sem["ev%d" % j], 1)
            q.dma_start(T.y[:, NC * j:NC * (j + 1)], T.yb[:, NC * j:NC * (j + 1)]).then_inc(sem[st], 16)
            stores[st] += 16
        g.sync.wait_ge(sem.sta, stores["sta"])
        g.scalar.wait_ge(sem.stb, stores["stb"])

    if total:
        g.wait_ge(sem.sent, total)
